import numpy as np
import ml_dtypes


def mxq(x, axis, fmt="e4m3"):
    dtype, down = {"e4m3": (ml_dtypes.float8_e4m3fn, 7), "e5m2": (ml_dtypes.float8_e5m2, 14)}[fmt]
    v = np.moveaxis(np.asarray(x, np.float32).astype(ml_dtypes.bfloat16).astype(np.float64), axis, -1)
    blocks = v.reshape(v.shape[:-1] + (-1, 32))
    amax = np.abs(blocks).max(-1, keepdims=True)
    byte = np.maximum(np.where(amax > 0, np.frexp(amax)[1] - 1 + 127, 0) - down, 1)
    scale = np.exp2(byte - 127.0)
    codes = (blocks / scale).astype(np.float32).astype(dtype).astype(np.float64)
    return np.moveaxis((codes * scale).reshape(v.shape), -1, axis)


WIDE = False


def mx_kscale(k):
    if not WIDE:
        return np.ones(k)
    levels = np.array([10, -10, 5, -5, 0])
    if k % 512:
        return np.exp2(np.random.permutation(np.resize(levels, k // 32))).repeat(32)
    a = np.empty((k // 512, 16))
    for p in range(k // 512):
        a[p, :8] = np.random.permutation(np.resize(levels, 8))
        for g in range(8):
            far = levels[np.abs(levels - a[p, g]) >= 10]
            a[p, g + 8] = far[np.random.randint(len(far))]
    return np.exp2(a.ravel()).repeat(32)


def f64(x):
    return np.asarray(x).astype(np.float64)


def striped(idx):
    return np.tile(idx.reshape(-1, 16).T, (8, 1)).astype(np.uint16)


def unstriped(offs):
    return offs[:16].T.reshape(-1).astype(np.int64)


def pack_weight(w):
    k, n = w.shape
    w = f64(np.asarray(w, np.float32).astype(ml_dtypes.bfloat16)).reshape(k // 32, 32, n)
    amax = np.abs(w).max(1)
    byte = np.clip(np.where(amax > 0, np.frexp(amax)[1] - 1 + 127 - 7, 1), 1, 254)
    scaled = (w * np.exp2(127.0 - byte)[:, None, :]).reshape(k, n).astype(np.float32)
    words = np.ascontiguousarray(scaled.reshape(k // 512, 128, 4, n).transpose(0, 1, 3, 2)).astype(ml_dtypes.float8_e4m3fn).view(np.uint8)
    return words, np.ascontiguousarray(byte.astype(np.uint8).reshape(k // 512, 16, n))


def unpack_weight(words, scales):
    g, p, n, _ = words.shape
    vals = np.ascontiguousarray(words).view(ml_dtypes.float8_e4m3fn).astype(np.float64) * np.repeat(np.exp2(scales.astype(np.float64) - 127.0), 8, axis=1)[..., None]
    return vals.transpose(0, 1, 3, 2).reshape(g * 512, n)


def gelu(v):
    return 0.5 * v * (1.0 + np.tanh(np.sqrt(2.0 / np.pi) * (v + 0.044715 * v**3)))


K, T, S, V, H, N = 1024, 2048, 1024, 512, 512, 128


def setup_inputs():
    n = np.random.standard_normal
    s = mx_kscale(K)[:, None]
    u = mx_kscale(H)
    packed_xT = pack_weight(n((K, T)) * s)
    return {
        "x_words": packed_xT[0],
        "x_scales": packed_xT[1],
        "w1": (n((K, H)) / np.sqrt(2 * K) / s * u).astype(np.float32),
        "w2": (n((K, H)) / np.sqrt(2 * K) / s * u).astype(np.float32),
        "w3": (n((H, N)) / np.sqrt(H) / u[:, None]).astype(np.float32),
        "offs": striped(np.random.permutation(T)[:S]),
        "cen": striped(np.random.permutation(S)[:V]),
        "pos1": striped(np.random.permutation(S)[:V]),
        "pos2": striped(np.random.permutation(S)[:V]),
    }


def reference(x_words, x_scales, w1, w2, w3, offs, cen, pos1, pos2):
    xq = unpack_weight(x_words, x_scales)[:, unstriped(offs)]
    y = mxq(f64(w1), 0, "e4m3").T @ xq
    yc = y[:, unstriped(cen)]
    e = mxq(f64(w2), 0, "e4m3").T @ xq
    z = np.maximum(gelu(yc + e[:, unstriped(pos1)]), gelu(yc + e[:, unstriped(pos2)]))
    return mxq(f64(w3), 0, "e4m3").T @ mxq(z, 0, "e4m3")

@@ -1,0 +1,260 @@
+from contextlib import ExitStack
+
+import concourse.mybir as mybir
+
+K, T, S, V, H, N = 1024, 2048, 1024, 512, 512, 128
+FLOPS = 2 * 2 * K * H * S + 2 * H * N * V
+
+F32 = mybir.dt.float32
+BF16 = mybir.dt.bfloat16
+I32 = mybir.dt.int32
+U32 = mybir.dt.uint32
+U16 = mybir.dt.uint16
+U8 = mybir.dt.uint8
+FP8X4 = mybir.dt.float8_e4m3fn_x4
+ADD = mybir.AluOpType.add
+MAX = mybir.AluOpType.max
+GELU = mybir.ActivationFunctionType.Gelu_apprx_tanh
+
+P = 128
+PACK = 4
+PASSES = K // (P * PACK)
+TILES = H // P
+BANK = 512
+HALVES = S // BANK
+LIST_ROWS = 16
+CHUNKS = [(0, 256), (256, 384), (384, 512)]
+
+
+def tile_picked_edgecv_gelu_p_kernel(
+    tc, x_words, x_scales, w1, w2, w3, offs, cen, pos1, pos2, out
+):
+    nc = tc.nc
+    with ExitStack() as ctx:
+        keep = ctx.enter_context(tc.tile_pool(name="keep", bufs=1))
+        psum = ctx.enter_context(tc.psum_pool(name="psum", bufs=8))
+
+        def load_list(source, name):
+            tile = keep.tile(list(source.shape), U16, name=name)
+            nc.sync.dma_start(tile[:], source)
+            return tile
+
+        def load_words(g):
+            tile = keep.tile([P, T], I32, name="x_table%d" % g)
+            nc.sync.dma_start(tile[:], x_words[g].rearrange("p n r -> p (n r)").bitcast(I32))
+            return tile
+
+        def load_weight(w, g, name):
+            tile = keep.tile([P, PACK, H], F32, name=name)
+            rows = w[g * P * PACK : (g + 1) * P * PACK, :]
+            nc.sync.dma_start(tile[:], rows.rearrange("(p j) c -> p j c", j=PACK))
+            return tile
+
+        scale_table = keep.tile([P, T], U8, name="scale_table")
+        nc.vector.memset(scale_table[:].bitcast(I32), 0)
+        zero_in = keep.tile([P, 1], F32, name="zero_in")
+        nc.vector.memset(zero_in[:], 0.0)
+
+        offs_sb = load_list(offs, "offs_sb")
+        w1_first = keep.tile([P, PACK, H], F32, name="w1_raw0")
+        w1_first_rows = w1[: P * PACK, :].rearrange("(p j) c -> p j c", j=PACK)
+        nc.sync.dma_start(w1_first[:, :2, :], w1_first_rows[:, :2, :])
+        for quad in range(4):
+            nc.sync.dma_start(
+                scale_table[32 * quad : 32 * quad + 4 * PASSES, :].bitcast(I32),
+                x_scales[:, 4 * quad : 4 * quad + 4, :].bitcast(I32),
+            )
+        zero = keep.tile([P, 1], F32, name="zero")
+        nc.scalar.activation(zero[:], zero_in[:], GELU)
+        x_table = [load_words(0)]
+        nc.sync.dma_start(w1_first[:, 2:, :], w1_first_rows[:, 2:, :])
+        w1_raw = [w1_first]
+        x_table.append(load_words(1))
+        w1_raw.append(load_weight(w1, 1, "w1_raw1"))
+        cen_sb = load_list(cen, "cen_sb")
+        w2_raw = [load_weight(w2, g, "w2_raw%d" % g) for g in range(PASSES)]
+        pos_sb = [load_list(pos1, "pos1_sb"), load_list(pos2, "pos2_sb")]
+        w3_raw = keep.tile([P, TILES, N], F32, name="w3_raw")
+        w3_rows = w3.rearrange("(q t c) n -> t q c n", t=TILES, c=4)
+        for t in range(TILES):
+            nc.sync.dma_start(w3_raw[:, t, :], w3_rows[t])
+
+        def deal(copy, raw, t, stage):
+            copy(
+                stage.rearrange("p (q c j) -> p q j c", c=4, j=PACK),
+                raw[:].rearrange("p j (q t c) -> p t q j c", t=TILES, c=4)[:, t],
+            )
+
+        def quantize(values, name, tag=None):
+            width = values.shape[1] // PACK
+            codes = keep.tile([P, width], U32, name=name + "_codes", tag=tag or name + "_codes", align_bytes=64)
+            scales = keep.tile([P, width], U8, name=name + "_scales", align_bytes=64)
+            nc.vector.quantize_mx(out=codes[:].bitcast(FP8X4), scales=scales[:], in_=values)
+            return codes, scales
+
+        def columns(weight, index):
+            cols = slice(index * P, (index + 1) * P)
+            return weight[0][:, cols], weight[1][:, cols]
+
+        x_scale = keep.tile([P, S], U8, name="x_scale", align_bytes=64)
+        x_codes = []
+
+        def gather_words(g, tag):
+            tile = keep.tile([P, S], U32, name="x_codes%d" % g, tag=tag, align_bytes=64)
+            nc.vector.tensor_copy(tile[:], x_table[g][:].bitcast(U32).indirect(offs_sb[:]))
+            x_codes.append(tile)
+
+        def product_pass(acc, weight, g, h):
+            codes, scales = weight
+            cols = slice(h * BANK, (h + 1) * BANK)
+            nc.tensor.matmul_mx(
+                out=acc[:],
+                lhsT=codes.bitcast(FP8X4),
+                lhsT_scale=scales,
+                rhs=x_codes[g][:, cols].bitcast(FP8X4),
+                rhs_scale=x_scale[4 * g : P, cols],
+                start=(g == 0),
+                stop=(g == PASSES - 1),
+            )
+
+        on_scalar, on_vector = nc.scalar.copy, nc.vector.tensor_copy
+        WIDE = P * PACK
+
+        nc.vector.tensor_copy(x_scale[:], scale_table[:].indirect(offs_sb[:]))
+        gather_words(0, "x_codes0")
+        early = keep.tile([P, 2 * WIDE], BF16, name="early", align_bytes=64)
+        third = keep.tile([P, WIDE], BF16, name="third", align_bytes=64)
+        last = keep.tile([P, PASSES * WIDE], BF16, name="last", align_bytes=64)
+        for t, room in enumerate([early[:, :WIDE], early[:, WIDE:], third[:], last[:, :WIDE]]):
+            deal(on_scalar, w1_raw[0], t, room)
+        y_acc = [[psum.tile([P, BANK], F32, name="acc") for h in range(HALVES)] for t in range(TILES)]
+
+        def run_pass(weight, index, g, t):
+            for h in range(HALVES):
+                product_pass(y_acc[t][h], columns(weight, index), g, h)
+
+        weight = quantize(early[:], "w1_early")
+        run_pass(weight, 0, 0, 0)
+        run_pass(weight, 1, 0, 1)
+        run_pass(quantize(third[:], "w1_third"), 0, 0, 2)
+        gather_words(1, "third")
+
+        y = [keep.tile([P, S], F32, name="y%d" % t, align_bytes=64) for t in range(TILES)]
+        e = [keep.tile([P, S], F32, name="e%d" % t) for t in range(TILES)]
+        edge = [keep.tile([P, TILES, V], F32, name="edge%d" % d, align_bytes=64) for d in range(2)]
+        stage1 = [keep.tile([P, WIDE], BF16, name="stage1_%d" % t, align_bytes=64) for t in range(TILES - 1)]
+        yc = {t: keep.tile([P, V], F32, name="yc%d" % t, align_bytes=64) for t in (0, 1, 3)}
+
+        def close_y(t, tag=None):
+            run_pass(quantize(stage1[t][:], "w1_1_%d" % t, tag), 0, 1, t)
+
+        def empty(copy, target, accs, h, lo=0, hi=BANK):
+            copy(target[:, h * BANK + lo : h * BANK + hi], accs[h][:, lo:hi])
+
+        def gather_centre(t):
+            nc.vector.tensor_copy(yc[t][:], y[t][:].indirect(cen_sb[:]))
+
+        def gather_edge(d, t, lo, hi):
+            picks = pos_sb[d][:, lo // LIST_ROWS : hi // LIST_ROWS]
+            nc.vector.tensor_tensor(edge[d][:, t, lo:hi], e[t][:].indirect(picks), yc[t][:, lo:hi], ADD)
+
+        stage2 = {1: yc[3][:].bitcast(BF16), 2: edge[1][:, 0, :].bitcast(BF16), 3: edge[1][:, 1, :].bitcast(BF16)}
+
+        def deal_w2(copy, g, t):
+            deal(copy, w2_raw[g], t, stage2[t][:, g * WIDE : (g + 1) * WIDE])
+
+        def make_e(t):
+            weight = quantize(stage2[t], "w2_%d" % t)
+            accs = []
+            for h in range(HALVES):
+                acc = psum.tile([P, BANK], F32, name="acc")
+                for g in range(PASSES):
+                    product_pass(acc, columns(weight, g), g, h)
+                accs.append(acc)
+            return accs
+
+        deal(on_scalar, w1_raw[1], 0, stage1[0][:])
+        deal(on_scalar, w1_raw[1], 1, stage1[1][:])
+        deal(on_vector, w1_raw[1], 2, stage1[2][:])
+        deal(on_vector, w1_raw[1], 3, last[:, WIDE:])
+        close_y(0)
+        close_y(1, "stage1_0")
+        close_y(2, "stage1_1")
+        weight = quantize(last[:], "w1_last", "stage1_2")
+        run_pass(weight, 0, 0, 3)
+        run_pass(weight, 1, 1, 3)
+        empty(on_scalar, y[0], y_acc[0], 0)
+        empty(on_scalar, y[0], y_acc[0], 1)
+        gather_centre(0)
+        for t in range(1, TILES):
+            for h in range(HALVES):
+                empty(on_scalar, y[t], y_acc[t], h)
+        first_stage = keep.tile([P, PASSES * WIDE], BF16, name="first_stage", tag="y0", align_bytes=64)
+        stage2[0] = first_stage[:]
+        deal_w2(on_vector, 0, 0)
+        gather_centre(1)
+        deal_w2(on_vector, 1, 0)
+        e_acc = [make_e(0)]
+        yc[2] = keep.tile([P, V], F32, name="yc2", tag="y0", align_bytes=64)
+        gather_centre(2)
+        for t in range(1, TILES):
+            deal_w2(on_scalar, 0, t)
+            deal_w2(on_scalar, 1, t)
+            e_acc.append(make_e(t))
+            if t == 1:
+                gather_centre(3)
+            if t < 3:
+                empty(on_scalar, e[t - 1], e_acc[t - 1], 0)
+                empty(on_scalar, e[t - 1], e_acc[t - 1], 1)
+                gather_edge(0, t - 1, 0, V)
+            if t > 1:
+                gather_edge(1, t - 2, 0, V)
+        empty(on_scalar, e[2], e_acc[2], 0)
+        empty(on_scalar, e[2], e_acc[2], 1, 0, 384)
+        empty(on_scalar, e[3], e_acc[3], 0)
+        empty(on_scalar, e[3], e_acc[3], 1)
+        empty(on_scalar, e[2], e_acc[2], 1, 384, BANK)
+
+        w3_dealt = keep.tile([P, N * PACK], BF16, name="w3_dealt", align_bytes=64)
+        on_scalar(
+            w3_dealt[:].rearrange("p (m i t) -> p m t i", i=4, t=TILES),
+            w3_raw[:].rearrange("p t (m i) -> p m t i", i=4),
+        )
+        w3_codes, w3_scales = quantize(w3_dealt[:], "w3")
+
+        act = [keep.tile([P, V * PACK], BF16, name="act%d" % d, align_bytes=64) for d in range(2)]
+
+        def activate(d, lo, hi):
+            nc.scalar.activation(
+                act[d][:, lo * PACK : hi * PACK].rearrange("p (v i t) -> p v t i", i=4, t=TILES),
+                edge[d][:, :, lo:hi].rearrange("p t (v i) -> p v t i", i=4),
+                GELU,
+                bias=zero[:],
+            )
+
+        for lo in range(0, V, V // 2):
+            gather_edge(0, 3, lo, lo + V // 2)
+            gather_edge(0, 2, lo, lo + V // 2)
+            activate(0, lo, lo + V // 2)
+        for lo, hi in CHUNKS:
+            gather_edge(1, 2, lo, hi)
+            gather_edge(1, 3, lo, hi)
+            activate(1, lo, hi)
+        for lo, hi in CHUNKS:
+            z = keep.tile([P, (hi - lo) * PACK], BF16, name="z%d" % lo, align_bytes=64)
+            cols = slice(lo * PACK, hi * PACK)
+            nc.vector.tensor_tensor(z[:], act[0][:, cols], act[1][:, cols], MAX)
+            codes, scales = quantize(z[:], "z%d" % lo)
+            acc = psum.tile([P, BANK], F32, name="acc")
+            nc.tensor.matmul_mx(
+                out=acc[:, : hi - lo],
+                lhsT=w3_codes[:].bitcast(FP8X4),
+                lhsT_scale=w3_scales[:],
+                rhs=codes[:].bitcast(FP8X4),
+                rhs_scale=scales[:],
+                start=True,
+                stop=True,
+            )
+            result = keep.tile([P, hi - lo], F32, name="result%d" % lo)
+            on_scalar(result[:], acc[:, : hi - lo])
+            nc.sync.dma_start(out[:, lo:hi], result[:])

@@ -59,11 +59,17 @@ def tile_picked_edgecv_gelu_p_kernel(
         w1_first = keep.tile([P, PACK, H], F32, name="w1_raw0")
         w1_first_rows = w1[: P * PACK, :].rearrange("(p j) c -> p j c", j=PACK)
         nc.sync.dma_start(w1_first[:, :2, :], w1_first_rows[:, :2, :])
-        for quad in range(4):
+        for quad in range(2):
             nc.sync.dma_start(
                 scale_table[32 * quad : 32 * quad + 4 * PASSES, :].bitcast(I32),
                 x_scales[:, 4 * quad : 4 * quad + 4, :].bitcast(I32),
             )
+        for quad in range(2, 4):
+            for g in range(PASSES):
+                nc.sync.dma_start(
+                    scale_table[32 * quad + 4 * g : 32 * quad + 4 * g + 4, :].bitcast(I32),
+                    x_scales[g, 4 * quad : 4 * quad + 4, :].bitcast(I32),
+                )
         zero = keep.tile([P, 1], F32, name="zero")
         nc.scalar.activation(zero[:], zero_in[:], GELU)
         x_table = [load_words(0)]
@@ -79,10 +85,10 @@ def tile_picked_edgecv_gelu_p_kernel(
         for t in range(TILES):
             nc.sync.dma_start(w3_raw[:, t, :], w3_rows[t])
 
-        def deal(copy, raw, t, stage):
+        def deal(copy, raw, t, stage, groups=slice(0, 32)):
             copy(
-                stage.rearrange("p (q c j) -> p q j c", c=4, j=PACK),
-                raw[:].rearrange("p j (q t c) -> p t q j c", t=TILES, c=4)[:, t],
+                stage.rearrange("p (q c j) -> p q j c", c=4, j=PACK)[:, groups],
+                raw[:].rearrange("p j (q t c) -> p t q j c", t=TILES, c=4)[:, t, groups],
             )
 
         def quantize(values, name, tag=None):
@@ -158,57 +164,66 @@ def tile_picked_edgecv_gelu_p_kernel(
             picks = pos_sb[d][:, lo // LIST_ROWS : hi // LIST_ROWS]
             nc.vector.tensor_tensor(edge[d][:, t, lo:hi], e[t][:].indirect(picks), yc[t][:, lo:hi], ADD)
 
-        stage2 = {1: yc[3][:].bitcast(BF16), 2: edge[1][:, 0, :].bitcast(BF16), 3: edge[1][:, 1, :].bitcast(BF16)}
+        stage2 = {1: yc[3][:].bitcast(BF16), 2: edge[1][:, 0, :].bitcast(BF16), 3: edge[0][:, 1, :].bitcast(BF16)}
 
         def deal_w2(copy, g, t):
             deal(copy, w2_raw[g], t, stage2[t][:, g * WIDE : (g + 1) * WIDE])
 
-        def make_e(t):
-            weight = quantize(stage2[t], "w2_%d" % t)
+        def multiply_e(weights):
             accs = []
             for h in range(HALVES):
                 acc = psum.tile([P, BANK], F32, name="acc")
                 for g in range(PASSES):
-                    product_pass(acc, columns(weight, g), g, h)
+                    product_pass(acc, weights[g], g, h)
                 accs.append(acc)
             return accs
 
-        deal(on_scalar, w1_raw[1], 0, stage1[0][:])
+        def make_e(t):
+            weight = quantize(stage2[t], "w2_%d" % t)
+            return multiply_e([columns(weight, g) for g in range(PASSES)])
+
+        deal(on_scalar, w1_raw[1], 0, stage1[0][:], slice(0, 16))
+        deal(on_vector, w1_raw[1], 0, stage1[0][:], slice(16, 32))
         deal(on_scalar, w1_raw[1], 1, stage1[1][:])
+        close_y(0)
         deal(on_vector, w1_raw[1], 2, stage1[2][:])
         deal(on_vector, w1_raw[1], 3, last[:, WIDE:])
-        close_y(0)
         close_y(1, "stage1_0")
         close_y(2, "stage1_1")
         weight = quantize(last[:], "w1_last", "stage1_2")
         run_pass(weight, 0, 0, 3)
         run_pass(weight, 1, 1, 3)
+        head_stage = keep.tile([P, WIDE], BF16, name="head_stage", align_bytes=64)
+        deal(on_vector, w2_raw[0], 0, head_stage[:])
+        w2_head = columns(quantize(head_stage[:], "w2_head"), 0)
         empty(on_scalar, y[0], y_acc[0], 0)
         empty(on_scalar, y[0], y_acc[0], 1)
         gather_centre(0)
         for t in range(1, TILES):
             for h in range(HALVES):
                 empty(on_scalar, y[t], y_acc[t], h)
-        first_stage = keep.tile([P, PASSES * WIDE], BF16, name="first_stage", tag="y0", align_bytes=64)
-        stage2[0] = first_stage[:]
-        deal_w2(on_vector, 0, 0)
+        next_stage = keep.tile([P, WIDE], BF16, name="next_stage", tag="y0", align_bytes=64)
+        deal(on_vector, w2_raw[1], 0, next_stage[:])
         gather_centre(1)
-        deal_w2(on_vector, 1, 0)
-        e_acc = [make_e(0)]
+        e_acc = [multiply_e([w2_head, columns(quantize(next_stage[:], "w2_next"), 0)])]
         yc[2] = keep.tile([P, V], F32, name="yc2", tag="y0", align_bytes=64)
         gather_centre(2)
-        for t in range(1, TILES):
+        deal_w2(on_scalar, 0, 1)
+        deal_w2(on_scalar, 1, 1)
+        e_acc.append(make_e(1))
+        gather_centre(3)
+        empty(on_scalar, e[0], e_acc[0], 0)
+        empty(on_scalar, e[0], e_acc[0], 1)
+        gather_edge(0, 0, 0, V)
+        for t in (2, 3):
             deal_w2(on_scalar, 0, t)
             deal_w2(on_scalar, 1, t)
             e_acc.append(make_e(t))
-            if t == 1:
-                gather_centre(3)
-            if t < 3:
-                empty(on_scalar, e[t - 1], e_acc[t - 1], 0)
-                empty(on_scalar, e[t - 1], e_acc[t - 1], 1)
-                gather_edge(0, t - 1, 0, V)
-            if t > 1:
-                gather_edge(1, t - 2, 0, V)
+        gather_edge(1, 0, 0, V)
+        empty(on_scalar, e[1], e_acc[1], 0)
+        empty(on_scalar, e[1], e_acc[1], 1)
+        gather_edge(0, 1, 0, V)
+        gather_edge(1, 1, 0, V)
         empty(on_scalar, e[2], e_acc[2], 0)
         empty(on_scalar, e[2], e_acc[2], 1, 0, 384)
         empty(on_scalar, e[3], e_acc[3], 0)
@@ -222,29 +237,35 @@ def tile_picked_edgecv_gelu_p_kernel(
         )
         w3_codes, w3_scales = quantize(w3_dealt[:], "w3")
 
-        act = [keep.tile([P, V * PACK], BF16, name="act%d" % d, align_bytes=64) for d in range(2)]
-
-        def activate(d, lo, hi):
+        def activate(target, d, lo, hi):
             nc.scalar.activation(
-                act[d][:, lo * PACK : hi * PACK].rearrange("p (v i t) -> p v t i", i=4, t=TILES),
+                target.rearrange("p (v i t) -> p v t i", i=4, t=TILES),
                 edge[d][:, :, lo:hi].rearrange("p t (v i) -> p v t i", i=4),
                 GELU,
                 bias=zero[:],
             )
 
+        act0 = keep.tile([P, V * PACK], BF16, name="act0", align_bytes=64)
         for lo in range(0, V, V // 2):
             gather_edge(0, 3, lo, lo + V // 2)
             gather_edge(0, 2, lo, lo + V // 2)
-            activate(0, lo, lo + V // 2)
+            activate(act0[:, lo * PACK : (lo + V // 2) * PACK], 0, lo, lo + V // 2)
+        act1 = []
         for lo, hi in CHUNKS:
             gather_edge(1, 2, lo, hi)
             gather_edge(1, 3, lo, hi)
-            activate(1, lo, hi)
-        for lo, hi in CHUNKS:
+            act1.append(keep.tile([P, (hi - lo) * PACK], BF16, name="act1_%d" % lo, align_bytes=64))
+            activate(act1[-1][:], 1, lo, hi)
+
+        def largest(index):
+            lo, hi = CHUNKS[index]
             z = keep.tile([P, (hi - lo) * PACK], BF16, name="z%d" % lo, align_bytes=64)
-            cols = slice(lo * PACK, hi * PACK)
-            nc.vector.tensor_tensor(z[:], act[0][:, cols], act[1][:, cols], MAX)
-            codes, scales = quantize(z[:], "z%d" % lo)
+            nc.vector.tensor_tensor(z[:], act0[:, lo * PACK : hi * PACK], act1[index][:], MAX)
+            return z
+
+        def project(index, z, tag=None):
+            lo, hi = CHUNKS[index]
+            codes, scales = quantize(z[:], "z%d" % lo, tag)
             acc = psum.tile([P, BANK], F32, name="acc")
             nc.tensor.matmul_mx(
                 out=acc[:, : hi - lo],
@@ -258,3 +279,10 @@ def tile_picked_edgecv_gelu_p_kernel(
             result = keep.tile([P, hi - lo], F32, name="result%d" % lo)
             on_scalar(result[:], acc[:, : hi - lo])
             nc.sync.dma_start(out[:, lo:hi], result[:])
+
+        z = largest(0)
+        for index in range(1, len(CHUNKS)):
+            z_next = largest(index)
+            project(index - 1, z, "act1_%d" % CHUNKS[index][0])
+            z = z_next
+        project(len(CHUNKS) - 1, z)

@@ -80,7 +80,8 @@ def tile_picked_edgecv_gelu_p_kernel(
         cen_sb = load_list(cen, "cen_sb")
         w2_raw = [load_weight(w2, g, "w2_raw%d" % g) for g in range(PASSES)]
         pos_sb = [load_list(pos1, "pos1_sb"), load_list(pos2, "pos2_sb")]
-        w3_raw = keep.tile([P, TILES, N], F32, name="w3_raw")
+        edge = [keep.tile([P, TILES, V], F32, name="edge%d" % d, align_bytes=64) for d in range(2)]
+        w3_raw = edge[1][:, 2, :].rearrange("p (t m) -> p t m", t=TILES)
         w3_rows = w3.rearrange("(q t c) n -> t q c n", t=TILES, c=4)
         for t in range(TILES):
             nc.sync.dma_start(w3_raw[:, t, :], w3_rows[t])
@@ -130,8 +131,8 @@ def tile_picked_edgecv_gelu_p_kernel(
         gather_words(0, "x_codes0")
         early = keep.tile([P, 2 * WIDE], BF16, name="early", align_bytes=64)
         third = keep.tile([P, WIDE], BF16, name="third", align_bytes=64)
-        last = keep.tile([P, PASSES * WIDE], BF16, name="last", align_bytes=64)
-        for t, room in enumerate([early[:, :WIDE], early[:, WIDE:], third[:], last[:, :WIDE]]):
+        rest = keep.tile([P, 4 * WIDE], BF16, name="rest", align_bytes=64)
+        for t, room in enumerate([early[:, :WIDE], early[:, WIDE:], third[:], rest[:, 2 * WIDE : 3 * WIDE]]):
             deal(on_scalar, w1_raw[0], t, room)
         y_acc = [[psum.tile([P, BANK], F32, name="acc") for h in range(HALVES)] for t in range(TILES)]
 
@@ -147,12 +148,8 @@ def tile_picked_edgecv_gelu_p_kernel(
 
         y = [keep.tile([P, S], F32, name="y%d" % t, align_bytes=64) for t in range(TILES)]
         e = [keep.tile([P, S], F32, name="e%d" % t) for t in range(TILES)]
-        edge = [keep.tile([P, TILES, V], F32, name="edge%d" % d, align_bytes=64) for d in range(2)]
-        stage1 = [keep.tile([P, WIDE], BF16, name="stage1_%d" % t, align_bytes=64) for t in range(TILES - 1)]
-        yc = {t: keep.tile([P, V], F32, name="yc%d" % t, align_bytes=64) for t in (0, 1, 3)}
-
-        def close_y(t, tag=None):
-            run_pass(quantize(stage1[t][:], "w1_1_%d" % t, tag), 0, 1, t)
+        first = keep.tile([P, WIDE], BF16, name="first", align_bytes=64)
+        yc = [keep.tile([P, V], F32, name="yc%d" % t, align_bytes=64) for t in range(TILES)]
 
         def empty(copy, target, accs, h, lo=0, hi=BANK):
             copy(target[:, h * BANK + lo : h * BANK + hi], accs[h][:, lo:hi])
@@ -164,49 +161,47 @@ def tile_picked_edgecv_gelu_p_kernel(
             picks = pos_sb[d][:, lo // LIST_ROWS : hi // LIST_ROWS]
             nc.vector.tensor_tensor(edge[d][:, t, lo:hi], e[t][:].indirect(picks), yc[t][:, lo:hi], ADD)
 
-        stage2 = {1: yc[3][:].bitcast(BF16), 2: edge[1][:, 0, :].bitcast(BF16), 3: edge[0][:, 1, :].bitcast(BF16)}
+        stage2 = {0: yc[2][:].bitcast(BF16), 1: yc[3][:].bitcast(BF16), 2: edge[1][:, 0, :].bitcast(BF16), 3: edge[1][:, 1, :].bitcast(BF16)}
 
         def deal_w2(copy, g, t):
             deal(copy, w2_raw[g], t, stage2[t][:, g * WIDE : (g + 1) * WIDE])
 
-        def multiply_e(weights):
+        def make_e(t):
+            weight = quantize(stage2[t], "w2_%d" % t)
             accs = []
             for h in range(HALVES):
                 acc = psum.tile([P, BANK], F32, name="acc")
                 for g in range(PASSES):
-                    product_pass(acc, weights[g], g, h)
+                    product_pass(acc, columns(weight, g), g, h)
                 accs.append(acc)
             return accs
 
-        def make_e(t):
-            weight = quantize(stage2[t], "w2_%d" % t)
-            return multiply_e([columns(weight, g) for g in range(PASSES)])
-
-        deal(on_scalar, w1_raw[1], 0, stage1[0][:], slice(0, 16))
-        deal(on_vector, w1_raw[1], 0, stage1[0][:], slice(16, 32))
-        deal(on_scalar, w1_raw[1], 1, stage1[1][:])
-        close_y(0)
-        deal(on_vector, w1_raw[1], 2, stage1[2][:])
-        deal(on_vector, w1_raw[1], 3, last[:, WIDE:])
-        close_y(1, "stage1_0")
-        close_y(2, "stage1_1")
-        weight = quantize(last[:], "w1_last", "stage1_2")
-        run_pass(weight, 0, 0, 3)
-        run_pass(weight, 1, 1, 3)
-        head_stage = keep.tile([P, WIDE], BF16, name="head_stage", align_bytes=64)
-        deal(on_vector, w2_raw[0], 0, head_stage[:])
-        w2_head = columns(quantize(head_stage[:], "w2_head"), 0)
-        empty(on_scalar, y[0], y_acc[0], 0)
-        empty(on_scalar, y[0], y_acc[0], 1)
-        gather_centre(0)
-        for t in range(1, TILES):
+        deal(on_scalar, w1_raw[1], 0, first[:], slice(0, 16))
+        deal(on_vector, w1_raw[1], 0, first[:], slice(16, 32))
+        deal(on_scalar, w1_raw[1], 1, rest[:, :WIDE])
+        run_pass(quantize(first[:], "w1_first"), 0, 1, 0)
+        deal(on_scalar, w1_raw[1], 2, rest[:, WIDE : 2 * WIDE])
+        deal(on_vector, w1_raw[1], 3, rest[:, 3 * WIDE :])
+        weight = quantize(rest[:], "w1_rest")
+        run_pass(weight, 0, 1, 1)
+        run_pass(weight, 1, 1, 2)
+        run_pass(weight, 2, 0, 3)
+        run_pass(weight, 3, 1, 3)
+        for g in range(PASSES):
+            nc.gpsimd.tensor_scalar(
+                stage2[0][:, g * WIDE : (g + 1) * WIDE].rearrange("p (q c j) -> p q c j", c=4, j=PACK),
+                w2_raw[g][:].rearrange("p j (q t c) -> p t q c j", t=TILES, c=4)[:, 0],
+                1.0,
+                0.0,
+                mybir.AluOpType.mult,
+                ADD,
+            )
+        for t in range(TILES):
             for h in range(HALVES):
                 empty(on_scalar, y[t], y_acc[t], h)
-        next_stage = keep.tile([P, WIDE], BF16, name="next_stage", tag="y0", align_bytes=64)
-        deal(on_vector, w2_raw[1], 0, next_stage[:])
+        gather_centre(0)
         gather_centre(1)
-        e_acc = [multiply_e([w2_head, columns(quantize(next_stage[:], "w2_next"), 0)])]
-        yc[2] = keep.tile([P, V], F32, name="yc2", tag="y0", align_bytes=64)
+        e_acc = [make_e(0)]
         gather_centre(2)
         deal_w2(on_scalar, 0, 1)
         deal_w2(on_scalar, 1, 1)
@@ -223,19 +218,17 @@ def tile_picked_edgecv_gelu_p_kernel(
         empty(on_scalar, e[1], e_acc[1], 0)
         empty(on_scalar, e[1], e_acc[1], 1)
         gather_edge(0, 1, 0, V)
-        gather_edge(1, 1, 0, V)
-        empty(on_scalar, e[2], e_acc[2], 0)
-        empty(on_scalar, e[2], e_acc[2], 1, 0, 384)
-        empty(on_scalar, e[3], e_acc[3], 0)
-        empty(on_scalar, e[3], e_acc[3], 1)
-        empty(on_scalar, e[2], e_acc[2], 1, 384, BANK)
+        for t in (2, 3):
+            empty(on_scalar, e[t], e_acc[t], 0)
+            empty(on_scalar, e[t], e_acc[t], 1)
+        gather_edge(0, 2, 0, V)
 
-        w3_dealt = keep.tile([P, N * PACK], BF16, name="w3_dealt", align_bytes=64)
+        w3_dealt = stage2[3][:, : N * PACK]
         on_scalar(
-            w3_dealt[:].rearrange("p (m i t) -> p m t i", i=4, t=TILES),
-            w3_raw[:].rearrange("p t (m i) -> p m t i", i=4),
+            w3_dealt.rearrange("p (m i t) -> p m t i", i=4, t=TILES),
+            w3_raw.rearrange("p t (m i) -> p m t i", i=4),
         )
-        w3_codes, w3_scales = quantize(w3_dealt[:], "w3")
+        w3_codes, w3_scales = quantize(w3_dealt, "w3")
 
         def activate(target, d, lo, hi):
             nc.scalar.activation(
@@ -248,12 +241,11 @@ def tile_picked_edgecv_gelu_p_kernel(
         act0 = keep.tile([P, V * PACK], BF16, name="act0", align_bytes=64)
         for lo in range(0, V, V // 2):
             gather_edge(0, 3, lo, lo + V // 2)
-            gather_edge(0, 2, lo, lo + V // 2)
             activate(act0[:, lo * PACK : (lo + V // 2) * PACK], 0, lo, lo + V // 2)
         act1 = []
         for lo, hi in CHUNKS:
-            gather_edge(1, 2, lo, hi)
-            gather_edge(1, 3, lo, hi)
+            for t in range(1, TILES):
+                gather_edge(1, t, lo, hi)
             act1.append(keep.tile([P, (hi - lo) * PACK], BF16, name="act1_%d" % lo, align_bytes=64))
             activate(act1[-1][:], 1, lo, hi)
 

from contextlib import ExitStack

import concourse.mybir as mybir

K, T, S, V, H, N = 1024, 2048, 1024, 512, 512, 128
FLOPS = 2 * 2 * K * H * S + 2 * H * N * V

F32 = mybir.dt.float32
BF16 = mybir.dt.bfloat16
I32 = mybir.dt.int32
U32 = mybir.dt.uint32
U16 = mybir.dt.uint16
U8 = mybir.dt.uint8
FP8X4 = mybir.dt.float8_e4m3fn_x4
ADD = mybir.AluOpType.add
MAX = mybir.AluOpType.max
GELU = mybir.ActivationFunctionType.Gelu_apprx_tanh

P = 128
PACK = 4
PASSES = K // (P * PACK)
TILES = H // P
BANK = 512
HALVES = S // BANK
LIST_ROWS = 16
CHUNKS = [(0, 256), (256, 384), (384, 512)]


def tile_picked_edgecv_gelu_p_kernel(
    tc, x_words, x_scales, w1, w2, w3, offs, cen, pos1, pos2, out
):
    nc = tc.nc
    with ExitStack() as ctx:
        keep = ctx.enter_context(tc.tile_pool(name="keep", bufs=1))
        psum = ctx.enter_context(tc.psum_pool(name="psum", bufs=8))

        def load_list(source, name):
            tile = keep.tile(list(source.shape), U16, name=name)
            nc.sync.dma_start(tile[:], source)
            return tile

        def load_words(g):
            tile = keep.tile([P, T], I32, name="x_table%d" % g)
            nc.sync.dma_start(tile[:], x_words[g].rearrange("p n r -> p (n r)").bitcast(I32))
            return tile

        def load_weight(w, g, name):
            tile = keep.tile([P, PACK, H], F32, name=name)
            rows = w[g * P * PACK : (g + 1) * P * PACK, :]
            nc.sync.dma_start(tile[:], rows.rearrange("(p j) c -> p j c", j=PACK))
            return tile

        scale_table = keep.tile([P, T], U8, name="scale_table")
        nc.vector.memset(scale_table[:].bitcast(I32), 0)
        zero_in = keep.tile([P, 1], F32, name="zero_in")
        nc.vector.memset(zero_in[:], 0.0)

        offs_sb = load_list(offs, "offs_sb")
        w1_first = keep.tile([P, PACK, H], F32, name="w1_raw0")
        w1_first_rows = w1[: P * PACK, :].rearrange("(p j) c -> p j c", j=PACK)
        nc.sync.dma_start(w1_first[:, :2, :], w1_first_rows[:, :2, :])
        for quad in range(2):
            nc.sync.dma_start(
                scale_table[32 * quad : 32 * quad + 4 * PASSES, :].bitcast(I32),
                x_scales[:, 4 * quad : 4 * quad + 4, :].bitcast(I32),
            )
        for quad in range(2, 4):
            for g in range(PASSES):
                nc.sync.dma_start(
                    scale_table[32 * quad + 4 * g : 32 * quad + 4 * g + 4, :].bitcast(I32),
                    x_scales[g, 4 * quad : 4 * quad + 4, :].bitcast(I32),
                )
        zero = keep.tile([P, 1], F32, name="zero")
        nc.scalar.activation(zero[:], zero_in[:], GELU)
        x_table = [load_words(0)]
        nc.sync.dma_start(w1_first[:, 2:, :], w1_first_rows[:, 2:, :])
        w1_raw = [w1_first]
        x_table.append(load_words(1))
        w1_raw.append(load_weight(w1, 1, "w1_raw1"))
        cen_sb = load_list(cen, "cen_sb")
        w2_raw = [load_weight(w2, g, "w2_raw%d" % g) for g in range(PASSES)]
        pos_sb = [load_list(pos1, "pos1_sb"), load_list(pos2, "pos2_sb")]
        edge = [keep.tile([P, TILES, V], F32, name="edge%d" % d, align_bytes=64) for d in range(2)]
        w3_raw = edge[1][:, 2, :].rearrange("p (t m) -> p t m", t=TILES)
        w3_rows = w3.rearrange("(q t c) n -> t q c n", t=TILES, c=4)
        for t in range(TILES):
            nc.sync.dma_start(w3_raw[:, t, :], w3_rows[t])

        def deal(copy, raw, t, stage, groups=slice(0, 32)):
            copy(
                stage.rearrange("p (q c j) -> p q j c", c=4, j=PACK)[:, groups],
                raw[:].rearrange("p j (q t c) -> p t q j c", t=TILES, c=4)[:, t, groups],
            )

        def quantize(values, name, tag=None):
            width = values.shape[1] // PACK
            codes = keep.tile([P, width], U32, name=name + "_codes", tag=tag or name + "_codes", align_bytes=64)
            scales = keep.tile([P, width], U8, name=name + "_scales", align_bytes=64)
            nc.vector.quantize_mx(out=codes[:].bitcast(FP8X4), scales=scales[:], in_=values)
            return codes, scales

        def columns(weight, index):
            cols = slice(index * P, (index + 1) * P)
            return weight[0][:, cols], weight[1][:, cols]

        x_scale = keep.tile([P, S], U8, name="x_scale", align_bytes=64)
        x_codes = []

        def gather_words(g, tag):
            tile = keep.tile([P, S], U32, name="x_codes%d" % g, tag=tag, align_bytes=64)
            nc.vector.tensor_copy(tile[:], x_table[g][:].bitcast(U32).indirect(offs_sb[:]))
            x_codes.append(tile)

        def product_pass(acc, weight, g, h):
            codes, scales = weight
            cols = slice(h * BANK, (h + 1) * BANK)
            nc.tensor.matmul_mx(
                out=acc[:],
                lhsT=codes.bitcast(FP8X4),
                lhsT_scale=scales,
                rhs=x_codes[g][:, cols].bitcast(FP8X4),
                rhs_scale=x_scale[4 * g : P, cols],
                start=(g == 0),
                stop=(g == PASSES - 1),
            )

        on_scalar, on_vector = nc.scalar.copy, nc.vector.tensor_copy
        WIDE = P * PACK

        nc.vector.tensor_copy(x_scale[:], scale_table[:].indirect(offs_sb[:]))
        gather_words(0, "x_codes0")
        early = keep.tile([P, 2 * WIDE], BF16, name="early", align_bytes=64)
        third = keep.tile([P, WIDE], BF16, name="third", align_bytes=64)
        rest = keep.tile([P, 4 * WIDE], BF16, name="rest", align_bytes=64)
        for t, room in enumerate([early[:, :WIDE], early[:, WIDE:], third[:], rest[:, 2 * WIDE : 3 * WIDE]]):
            deal(on_scalar, w1_raw[0], t, room)
        y_acc = [[psum.tile([P, BANK], F32, name="acc") for h in range(HALVES)] for t in range(TILES)]

        def run_pass(weight, index, g, t):
            for h in range(HALVES):
                product_pass(y_acc[t][h], columns(weight, index), g, h)

        weight = quantize(early[:], "w1_early")
        run_pass(weight, 0, 0, 0)
        run_pass(weight, 1, 0, 1)
        run_pass(quantize(third[:], "w1_third"), 0, 0, 2)
        gather_words(1, "third")

        y = [keep.tile([P, S], F32, name="y%d" % t, align_bytes=64) for t in range(TILES)]
        e = [keep.tile([P, S], F32, name="e%d" % t) for t in range(TILES)]
        first = keep.tile([P, WIDE], BF16, name="first", align_bytes=64)
        yc = [keep.tile([P, V], F32, name="yc%d" % t, align_bytes=64) for t in range(TILES)]

        def empty(copy, target, accs, h, lo=0, hi=BANK):
            copy(target[:, h * BANK + lo : h * BANK + hi], accs[h][:, lo:hi])

        def gather_centre(t):
            nc.vector.tensor_copy(yc[t][:], y[t][:].indirect(cen_sb[:]))

        def gather_edge(d, t, lo, hi):
            picks = pos_sb[d][:, lo // LIST_ROWS : hi // LIST_ROWS]
            nc.vector.tensor_tensor(edge[d][:, t, lo:hi], e[t][:].indirect(picks), yc[t][:, lo:hi], ADD)

        stage2 = {0: yc[2][:].bitcast(BF16), 1: yc[3][:].bitcast(BF16), 2: edge[1][:, 0, :].bitcast(BF16), 3: edge[1][:, 1, :].bitcast(BF16)}

        def deal_w2(copy, g, t):
            deal(copy, w2_raw[g], t, stage2[t][:, g * WIDE : (g + 1) * WIDE])

        def make_e(t):
            weight = quantize(stage2[t], "w2_%d" % t)
            accs = []
            for h in range(HALVES):
                acc = psum.tile([P, BANK], F32, name="acc")
                for g in range(PASSES):
                    product_pass(acc, columns(weight, g), g, h)
                accs.append(acc)
            return accs

        deal(on_scalar, w1_raw[1], 0, first[:], slice(0, 16))
        deal(on_vector, w1_raw[1], 0, first[:], slice(16, 32))
        deal(on_scalar, w1_raw[1], 1, rest[:, :WIDE])
        run_pass(quantize(first[:], "w1_first"), 0, 1, 0)
        deal(on_scalar, w1_raw[1], 2, rest[:, WIDE : 2 * WIDE])
        deal(on_vector, w1_raw[1], 3, rest[:, 3 * WIDE :])
        weight = quantize(rest[:], "w1_rest")
        run_pass(weight, 0, 1, 1)
        run_pass(weight, 1, 1, 2)
        run_pass(weight, 2, 0, 3)
        run_pass(weight, 3, 1, 3)
        for g in range(PASSES):
            nc.gpsimd.tensor_scalar(
                stage2[0][:, g * WIDE : (g + 1) * WIDE].rearrange("p (q c j) -> p q c j", c=4, j=PACK),
                w2_raw[g][:].rearrange("p j (q t c) -> p t q c j", t=TILES, c=4)[:, 0],
                1.0,
                0.0,
                mybir.AluOpType.mult,
                ADD,
            )
        for t in range(TILES):
            for h in range(HALVES):
                empty(on_scalar, y[t], y_acc[t], h)
        gather_centre(0)
        gather_centre(1)
        e_acc = [make_e(0)]
        gather_centre(2)
        deal_w2(on_scalar, 0, 1)
        deal_w2(on_scalar, 1, 1)
        e_acc.append(make_e(1))
        gather_centre(3)
        empty(on_scalar, e[0], e_acc[0], 0)
        empty(on_scalar, e[0], e_acc[0], 1)
        gather_edge(0, 0, 0, V)
        for t in (2, 3):
            deal_w2(on_scalar, 0, t)
            deal_w2(on_scalar, 1, t)
            e_acc.append(make_e(t))
        gather_edge(1, 0, 0, V)
        empty(on_scalar, e[1], e_acc[1], 0)
        empty(on_scalar, e[1], e_acc[1], 1)
        gather_edge(0, 1, 0, V)
        for t in (2, 3):
            empty(on_scalar, e[t], e_acc[t], 0)
            empty(on_scalar, e[t], e_acc[t], 1)
        gather_edge(0, 2, 0, V)

        w3_dealt = stage2[3][:, : N * PACK]
        on_scalar(
            w3_dealt.rearrange("p (m i t) -> p m t i", i=4, t=TILES),
            w3_raw.rearrange("p t (m i) -> p m t i", i=4),
        )
        w3_codes, w3_scales = quantize(w3_dealt, "w3")

        def activate(target, d, lo, hi):
            nc.scalar.activation(
                target.rearrange("p (v i t) -> p v t i", i=4, t=TILES),
                edge[d][:, :, lo:hi].rearrange("p t (v i) -> p v t i", i=4),
                GELU,
                bias=zero[:],
            )

        act0 = keep.tile([P, V * PACK], BF16, name="act0", align_bytes=64)
        for lo in range(0, V, V // 2):
            gather_edge(0, 3, lo, lo + V // 2)
            activate(act0[:, lo * PACK : (lo + V // 2) * PACK], 0, lo, lo + V // 2)
        act1 = []
        for lo, hi in CHUNKS:
            for t in range(1, TILES):
                gather_edge(1, t, lo, hi)
            act1.append(keep.tile([P, (hi - lo) * PACK], BF16, name="act1_%d" % lo, align_bytes=64))
            activate(act1[-1][:], 1, lo, hi)

        def largest(index):
            lo, hi = CHUNKS[index]
            z = keep.tile([P, (hi - lo) * PACK], BF16, name="z%d" % lo, align_bytes=64)
            nc.vector.tensor_tensor(z[:], act0[:, lo * PACK : hi * PACK], act1[index][:], MAX)
            return z

        def project(index, z, tag=None):
            lo, hi = CHUNKS[index]
            codes, scales = quantize(z[:], "z%d" % lo, tag)
            acc = psum.tile([P, BANK], F32, name="acc")
            nc.tensor.matmul_mx(
                out=acc[:, : hi - lo],
                lhsT=w3_codes[:].bitcast(FP8X4),
                lhsT_scale=w3_scales[:],
                rhs=codes[:].bitcast(FP8X4),
                rhs_scale=scales[:],
                start=True,
                stop=True,
            )
            result = keep.tile([P, hi - lo], F32, name="result%d" % lo)
            on_scalar(result[:], acc[:, : hi - lo])
            nc.sync.dma_start(out[:, lo:hi], result[:])

        z = largest(0)
        for index in range(1, len(CHUNKS)):
            z_next = largest(index)
            project(index - 1, z, "act1_%d" % CHUNKS[index][0])
            z = z_next
        project(len(CHUNKS) - 1, z)
